import numpy as np, ml_dtypes
CORES = [100,101,102,103,108,109,110,111]
N = 8
import mx_ref
NC, KT, WT = 128, 8, 1
BF = ml_dtypes.bfloat16
def cut(t, i, w=512):
    return t[:, w * i:w * i + w]
def pk(c, s, i=0):
    return (np.ascontiguousarray(c[:, 512 * i:512 * i + 512]), mx_ref.live(s[:, 128 * i:128 * i + 128]))
def inputs(rng, e, E):
    def f(*shape):
        v = (rng.standard_normal(shape, dtype=np.float32) * np.exp2(rng.integers(-2, 3, shape[:-1] + (1,)))).astype(BF)
        return mx_ref.spread((v.astype(np.float32) * np.exp2(rng.integers(-E, E + 1, shape[:-2] + (1, 1))).astype(np.float32)).astype(BF), rng, e)
    def packed(k):
        c = np.zeros((N, 128, k * 512), np.uint8); s = np.zeros((N, 128, k * 128), np.uint8)
        for r in range(N):
            for i in range(k):
                a, b = mx_ref.quantize(f(128, 512)); c[r][:, 512 * i:512 * i + 512] = a; s[r][:, 128 * i:128 * i + 128] = mx_ref.plane(b, rng)
        return c, s
    d = {}
    d["wc"], d["ws"] = packed(KT * WT)
    d["x"] = f(N, 128, KT * 4 * NC)
    return d
def setup_inputs(rng):
    return inputs(rng, 0, 0)
def setup_inputs_blocks(rng):
    return inputs(rng, 2, 0)
def setup_inputs_wide(rng):
    d = inputs(rng, 0, 1); d["x"] = inputs(rng, 0, 0)["x"]
    return d
def reference(wc, ws, x):
    X = [[mx_ref.quantize(cut(x[j], t, 4 * NC)) for t in range(KT)] for j in range(N)]
    y = np.zeros((N, 128, N * WT * NC), np.float32)
    for r in range(N):
        for b in range(N * WT):
            j, i = divmod(b, WT)
            for t in range(KT):
                p = mx_ref.matmul(pk(wc[r], ws[r], KT * i + t), X[j][t])
                z = p if t == 0 else z + p
            y[r][:, NC * b:NC * b + NC] = z
    return {"y": y}

@@ -1,0 +1,237 @@
+from concourse.bass import DstId, RemoteDMATransfer
+from concourse.mybir import dt
+
+CODES = "float8_e4m3fn_x4"
+N = 8
+SIM_CORES = 112
+PL = 2
+SEQ = (0, PL, 1)
+
+SCRATCH = {
+    "w": ("sbuf", [128, 1024], CODES), "wp": ("sbuf", [128, 1024], "uint8"),
+    "own": ("sbuf", [128, 1024], CODES), "ownp": ("sbuf", [128, 1024], "uint8"),
+    "xin": ("sbuf", [128, 2048], "bfloat16"),
+    "sb": ("sbuf", [128, 512], CODES), "sbp": ("sbuf", [128, 512], "uint8"),
+    "yst": ("sbuf", [128, 256], "float32"),
+    "ps": ("psum", [128, 4096], "float32"),
+}
+for _j in range(N):
+    SCRATCH["lc%d_0" % _j] = ("dram", [128, 512], CODES)
+    SCRATCH["lc%d_1" % _j] = ("dram", [128, 512], CODES)
+    SCRATCH["lp%d" % _j] = ("dram", [128, 1024], "uint8")
+
+SEMAPHORES = (["a%d_%d" % (j, p) for j in range(N) for p in range(3)]
+              + ["s0", "s1", "s2", "sf", "wl"]
+              + ["xl%d" % i for i in range(4)] + ["q%d" % i for i in range(4)]
+              + ["f0", "f1", "f2", "e0", "e1", "e2", "yc0", "yc1", "ys0", "ys1"])
+
+
+def ones(mask):
+    return bin(mask).count("1")
+
+
+def layout(T, topo):
+    out = {}
+    for ch in sorted(set(topo.chip(c) for c in T.cores)):
+        far = [c for c in T.cores if topo.chip(c) != ch]
+
+        def gate(c):
+            return all(topo.may_write(c, d) for d in far)
+        mine = [c for c in T.cores if topo.chip(c) == ch]
+        rest = [c for c in range(SIM_CORES) if topo.chip(c) == ch and c not in mine]
+        out[ch] = ([c for c in mine if not gate(c)], [c for c in mine if gate(c)],
+                   [c for c in rest if not gate(c)], [c for c in rest if gate(c)])
+    return out
+
+
+def build_plan(T, topo, lay):
+    plan = {}
+    way = {}
+
+    def put(src, j, p, dsts, mask):
+        plan.setdefault(src, []).append((j, p, dsts, mask))
+        for d in dsts:
+            way[(d, j, p)] = mask
+    for ch in lay:
+        far = [c for c in lay if c != ch][0]
+        inner, gates = lay[ch][0], lay[ch][1]
+        ranks, franks = inner + gates, lay[far][0] + lay[far][1]
+        for src in ranks:
+            j = T.rank_of(src)
+            peers = [c for c in ranks if c != src]
+            on = topo.mask(src, peers[0])
+            if src in gates:
+                k = gates.index(src)
+                gate, land = src, lay[far][0][k]
+                cross = topo.mask(gate, land)
+            else:
+                k = inner.index(src)
+                gate, land = gates[k], lay[far][2][k]
+                cross = topo.mask(gate, land)
+                peers = [gate] + [c for c in peers if c != gate]
+            fw = [c for c in franks if c != land]
+            for p in SEQ:
+                if gate == src:
+                    put(src, j, p, [land], cross)
+                    put(src, j, p, peers, on & ~cross)
+                else:
+                    put(src, j, p, peers, on)
+                    put(gate, j, p, [land], cross)
+                put(land, j, p, fw, topo.mask(land, fw[0]))
+    return plan, way
+
+
+def rank_program(g, core, T, topo):
+    lay = layout(T, topo)
+    plan, way = build_plan(T, topo, lay)
+    mine = plan.get(core, [])
+    rank = T.rank_of(core)
+    if not mine:
+        return
+    sem = T.sem
+    chip = topo.chip(core)
+
+    def place(j):
+        c = T.cores[j]
+        return (topo.chip(c) != chip, c in lay[topo.chip(c)][0])
+
+    def land(j, p):
+        return T["lp%d" % j][:, :] if p == PL else T["lc%d_%d" % (j, p)][:, :].bitcast(dt.uint8)
+
+    def source(j, p):
+        if j != rank:
+            return land(j, p)
+        return T.ownp[:, :] if p == PL else T.own[:, 512 * p:512 * p + 512].bitcast(dt.uint8)
+
+    def dst_id(c):
+        a = topo.addr(c)
+        return DstId(rid=a[0], pnc=a[1])
+
+    def arrived(q, j, p):
+        q.wait_ge(sem["a%d_%d" % (j, p)], ones(way[(core, j, p)]))
+
+    def quantised(q, half):
+        q.wait_ge(sem["q%d" % (2 * half)], 2)
+        q.wait_ge(sem["q%d" % (2 * half + 1)], 2)
+
+    def stage(i):
+        j, p = mine[i][0], mine[i][1]
+        far, inner = place(j)
+        hop = 0 if j == rank else 1.5 if not far else 3.6 if inner else 2.6
+        return (SEQ.index(p) + hop, i)
+    groups = []
+    for i in sorted(range(len(mine)), key=stage):
+        j, p, dsts, mask = mine[i]
+        if groups and groups[-1][0] == (j, p):
+            groups[-1][1].append((dsts, mask))
+        else:
+            groups.append(((j, p), [(dsts, mask)]))
+    sent = [0, 0, 0]
+    passed = 0
+    for (j, p), trs in groups:
+        total = sum(ones(m) for (d, m) in trs)
+        if j == rank:
+            quantised(g, 0 if p == 0 else 1)
+            if p == PL:
+                quantised(g, 0)
+            sent[p] += total
+            ls = sem["s%d" % p]
+        else:
+            arrived(g, j, p)
+            passed += total
+            ls = sem.sf
+        g.remote_dma_fused([RemoteDMATransfer(
+            dst_ids=[dst_id(d) for d in dsts], dma_engine_mask=m, remote_sem=sem["a%d_%d" % (j, p)],
+            srcs=[source(j, p)], dsts=[land(j, p) for d in dsts]) for (dsts, m) in trs], local_sem=ls)
+    if passed:
+        g.wait_ge(sem.sf, passed)
+    if rank is None:
+        return
+
+    for i in range(4):
+        q = g.sync if i % 2 == 0 else g.scalar
+        h = 1024 * (i % 2)
+        if i == 2:
+            g.scalar.dma_start(T.wp[:, :], T.ws[:, :]).then_inc(sem.wl, 16)
+            g.sync.dma_start(T.w[:, :].bitcast(dt.uint8), T.wc[:, :]).then_inc(sem.wl, 16)
+        if i >= 2:
+            q.wait_ge(sem["q%d" % (i - 2)], 2)
+        q.dma_start(T.xin[:, h:h + 1024], T.x[:, 1024 * i:1024 * i + 1024]).then_inc(sem["xl%d" % i], 16)
+    for i in range(4):
+        g.vector.wait_ge(sem["xl%d" % i], 16)
+        for t in (2 * i, 2 * i + 1):
+            g.vector.quantize_mx(T.own[:, 128 * t:128 * t + 128], T.ownp[:, 128 * t:128 * t + 128],
+                                 T.xin[:, 512 * (t % 4):512 * (t % 4) + 512]).then_inc(sem["q%d" % i], 1)
+
+    def order(x):
+        j, c = x
+        far, inner = place(j)
+        return (far, inner if far else 0, c, (inner, j) if far else (not inner, j))
+    items = sorted([(j, c) for j in range(N) for c in range(2) if j != rank], key=order)
+    slots = [(T.sb, T.sbp, 0), (T.own, T.ownp, 0), (T.own, T.ownp, 512)]
+    free = [0, 1, 1]
+    full = [0, 0, 0]
+    halves = [0] * N
+    count = [0]
+
+    def products(j, c, s):
+        codes, planes, col = slots[s]
+        halves[j] += 1
+        for u in range(4):
+            a, b = 128 * (4 * c + u), col + 128 * u
+            ins = g.tensor.matmul_mx(T.ps[:, 512 * j:512 * j + 128], T.w[:, a:a + 128], T.wp[:, a:a + 128],
+                                     codes[:, b:b + 128], planes[:, b:b + 128],
+                                     halves[j] == 1 and u == 0, halves[j] == 2 and u == 3)
+        ins.then_inc(sem["f%d" % s], 1)
+
+    def collect(j, s):
+        n = count[0]
+        count[0] = n + 1
+        h = n % 2
+        g.vector.wait_ge(sem["f%d" % s], free[s])
+        if n >= 2:
+            g.vector.wait_ge(sem["ys%d" % h], 16 * (n // 2))
+        g.vector.tensor_copy(T.yst[:, 128 * h:128 * h + 128], T.ps[:, 512 * j:512 * j + 128]).then_inc(sem["yc%d" % h], 1)
+        return n
+
+    def store(j, n):
+        h = n % 2
+        g.scalar.wait_ge(sem["yc%d" % h], n // 2 + 1)
+        g.scalar.dma_start(T.y[:, 128 * j:128 * j + 128], T.yst[:, 128 * h:128 * h + 128]).then_inc(sem["ys%d" % h], 16)
+
+    g.tensor.wait_ge(sem.wl, 32)
+    quantised(g.tensor, 0)
+    products(rank, 0, 1)
+    quantised(g.tensor, 1)
+    products(rank, 1, 2)
+    store(rank, collect(rank, 2))
+    pend = []
+    for i, (j, c) in enumerate(items):
+        s = i % 3
+        codes, planes, col = slots[s]
+        for q in (g.sync, g.scalar):
+            if free[s]:
+                q.wait_ge(sem["f%d" % s], free[s])
+            if s and i < 3:
+                q.wait_ge(sem["s%d" % (s - 1)], sent[s - 1])
+                q.wait_ge(sem["s%d" % PL], sent[PL])
+        arrived(g.sync, j, c)
+        g.sync.dma_start(codes[:, col:col + 512].bitcast(dt.uint8), land(j, c)).then_inc(sem["e%d" % s], 16)
+        arrived(g.scalar, j, PL)
+        g.scalar.dma_start(planes[:, col:col + 512], T["lp%d" % j][:, 512 * c:512 * c + 512]).then_inc(sem["e%d" % s], 16)
+        while pend and pend[0][2] + 3 <= i:
+            store(pend[0][0], pend[0][1])
+            pend.pop(0)
+        full[s] += 32
+        g.tensor.wait_ge(sem["e%d" % s], full[s])
+        products(j, c, s)
+        free[s] += 1
+        if halves[j] == 2:
+            pend.append((j, collect(j, s), i))
+    for (j, n, i) in pend:
+        store(j, n)
+    for q in (g.vector, g.scalar):
+        q.wait_ge(sem.ys0, 16 * ((N + 1) // 2))
+        q.wait_ge(sem.ys1, 16 * (N // 2))
+    for s in range(3):
+        g.vector.wait_ge(sem["f%d" % s], free[s])

@@ -4,24 +4,24 @@ from concourse.mybir import dt
 CODES = "float8_e4m3fn_x4"
 N = 8
 SIM_CORES = 112
-PL = 2
-SEQ = (0, PL, 1)
+C0, PL, C1 = 0, 1, 2
+PIECES = (C0, PL, C1)
 
 SCRATCH = {
     "w": ("sbuf", [128, 1024], CODES), "wp": ("sbuf", [128, 1024], "uint8"),
     "own": ("sbuf", [128, 1024], CODES), "ownp": ("sbuf", [128, 1024], "uint8"),
-    "xin": ("sbuf", [128, 2048], "bfloat16"),
     "sb": ("sbuf", [128, 512], CODES), "sbp": ("sbuf", [128, 512], "uint8"),
+    "xin": ("sbuf", [128, 2048], "bfloat16"),
     "yst": ("sbuf", [128, 256], "float32"),
     "ps": ("psum", [128, 4096], "float32"),
 }
 for _j in range(N):
-    SCRATCH["lc%d_0" % _j] = ("dram", [128, 512], CODES)
-    SCRATCH["lc%d_1" % _j] = ("dram", [128, 512], CODES)
+    SCRATCH["lc%d_%d" % (_j, C0)] = ("dram", [128, 512], CODES)
+    SCRATCH["lc%d_%d" % (_j, C1)] = ("dram", [128, 512], CODES)
     SCRATCH["lp%d" % _j] = ("dram", [128, 1024], "uint8")
 
-SEMAPHORES = (["a%d_%d" % (j, p) for j in range(N) for p in range(3)]
-              + ["s0", "s1", "s2", "sf", "wl"]
+SEMAPHORES = (["a%d_%d" % (j, p) for j in range(N) for p in PIECES]
+              + ["s%d" % p for p in PIECES] + ["sf", "wl"]
               + ["xl%d" % i for i in range(4)] + ["q%d" % i for i in range(4)]
               + ["f0", "f1", "f2", "e0", "e1", "e2", "yc0", "yc1", "ys0", "ys1"])
 
@@ -44,64 +44,66 @@ def layout(T, topo):
     return out
 
 
+def first_of(T, topo, core):
+    ranks = [c for c in T.cores if topo.chip(c) == topo.chip(core)]
+    return ranks[(ranks.index(core) + 1) % len(ranks)]
+
+
 def build_plan(T, topo, lay):
     plan = {}
     way = {}
 
-    def put(src, j, p, dsts, mask):
-        plan.setdefault(src, []).append((j, p, dsts, mask))
-        for d in dsts:
-            way[(d, j, p)] = mask
+    def put(src, j, p, hop, trs):
+        plan.setdefault(src, []).append((j, p, hop, trs))
+        for dsts, mask in trs:
+            for d in dsts:
+                way[(d, j, p)] = mask
     for ch in lay:
         far = [c for c in lay if c != ch][0]
-        inner, gates = lay[ch][0], lay[ch][1]
+        inner, gates, _, ghelp = lay[ch]
         ranks, franks = inner + gates, lay[far][0] + lay[far][1]
         for src in ranks:
             j = T.rank_of(src)
             peers = [c for c in ranks if c != src]
             on = topo.mask(src, peers[0])
-            if src in gates:
-                k = gates.index(src)
-                gate, land = src, lay[far][0][k]
-                cross = topo.mask(gate, land)
-            else:
-                k = inner.index(src)
-                gate, land = gates[k], lay[far][2][k]
-                cross = topo.mask(gate, land)
-                peers = [gate] + [c for c in peers if c != gate]
-            fw = [c for c in franks if c != land]
-            for p in SEQ:
-                if gate == src:
-                    put(src, j, p, [land], cross)
-                    put(src, j, p, peers, on & ~cross)
+            k = (gates if src in gates else inner).index(src)
+            for p in PIECES:
+                if src in gates:
+                    land = lay[far][0 if p == C1 else 2][k]
+                    cross = topo.mask(src, land)
+                    put(src, j, p, 0, [([land, peers[0]], cross), (peers[1:], on & ~cross)])
+                    hop = 1.05
                 else:
-                    put(src, j, p, peers, on)
-                    put(gate, j, p, [land], cross)
-                put(land, j, p, fw, topo.mask(land, fw[0]))
+                    via, land = ghelp[k], lay[far][2][k]
+                    put(src, j, p, 0, [([via] + peers, on)])
+                    put(via, j, p, 1, [([land], topo.mask(via, land))])
+                    hop = 2
+                to = [c for c in franks if c != land]
+                put(land, j, p, hop, [(to, topo.mask(land, to[0]))])
     return plan, way
 
 
 def rank_program(g, core, T, topo):
     lay = layout(T, topo)
     plan, way = build_plan(T, topo, lay)
-    mine = plan.get(core, [])
-    rank = T.rank_of(core)
-    if not mine:
+    if core not in plan:
         return
+    rank = T.rank_of(core)
     sem = T.sem
     chip = topo.chip(core)
 
-    def place(j):
-        c = T.cores[j]
-        return (topo.chip(c) != chip, c in lay[topo.chip(c)][0])
-
-    def land(j, p):
+    def dram(j, p):
         return T["lp%d" % j][:, :] if p == PL else T["lc%d_%d" % (j, p)][:, :].bitcast(dt.uint8)
 
     def source(j, p):
         if j != rank:
-            return land(j, p)
-        return T.ownp[:, :] if p == PL else T.own[:, 512 * p:512 * p + 512].bitcast(dt.uint8)
+            return dram(j, p)
+        return T.ownp[:, :] if p == PL else T.own[:, 256 * p:256 * p + 512].bitcast(dt.uint8)
+
+    def land(d, j, p):
+        if p == C0 and T.rank_of(d) is not None and first_of(T, topo, d) == T.cores[j]:
+            return T.sb[:, :].bitcast(dt.uint8)
+        return dram(j, p)
 
     def dst_id(c):
         a = topo.addr(c)
@@ -114,26 +116,14 @@ def rank_program(g, core, T, topo):
         q.wait_ge(sem["q%d" % (2 * half)], 2)
         q.wait_ge(sem["q%d" % (2 * half + 1)], 2)
 
-    def stage(i):
-        j, p = mine[i][0], mine[i][1]
-        far, inner = place(j)
-        hop = 0 if j == rank else 1.5 if not far else 3.6 if inner else 2.6
-        return (SEQ.index(p) + hop, i)
-    groups = []
-    for i in sorted(range(len(mine)), key=stage):
-        j, p, dsts, mask = mine[i]
-        if groups and groups[-1][0] == (j, p):
-            groups[-1][1].append((dsts, mask))
-        else:
-            groups.append(((j, p), [(dsts, mask)]))
-    sent = [0, 0, 0]
+    sent = {p: 0 for p in PIECES}
     passed = 0
-    for (j, p), trs in groups:
+    for j, p, hop, trs in sorted(plan[core], key=lambda w: (w[1] + 1.6 * w[2], w[0])):
         total = sum(ones(m) for (d, m) in trs)
         if j == rank:
-            quantised(g, 0 if p == 0 else 1)
-            if p == PL:
-                quantised(g, 0)
+            quantised(g, 0)
+            if p != C0:
+                quantised(g, 1)
             sent[p] += total
             ls = sem["s%d" % p]
         else:
@@ -142,7 +132,7 @@ def rank_program(g, core, T, topo):
             ls = sem.sf
         g.remote_dma_fused([RemoteDMATransfer(
             dst_ids=[dst_id(d) for d in dsts], dma_engine_mask=m, remote_sem=sem["a%d_%d" % (j, p)],
-            srcs=[source(j, p)], dsts=[land(j, p) for d in dsts]) for (dsts, m) in trs], local_sem=ls)
+            srcs=[source(j, p)], dsts=[land(d, j, p) for d in dsts]) for (dsts, m) in trs], local_sem=ls)
     if passed:
         g.wait_ge(sem.sf, passed)
     if rank is None:
@@ -163,16 +153,20 @@ def rank_program(g, core, T, topo):
             g.vector.quantize_mx(T.own[:, 128 * t:128 * t + 128], T.ownp[:, 128 * t:128 * t + 128],
                                  T.xin[:, 512 * (t % 4):512 * (t % 4) + 512]).then_inc(sem["q%d" % i], 1)
 
+    first = T.rank_of(first_of(T, topo, core))
+
     def order(x):
         j, c = x
-        far, inner = place(j)
-        return (far, inner if far else 0, c, (inner, j) if far else (not inner, j))
+        inner = T.cores[j] in lay[topo.chip(T.cores[j])][0]
+        if topo.chip(T.cores[j]) != chip:
+            return (1, inner, j, c)
+        return (0, j != first, c, inner, j)
     items = sorted([(j, c) for j in range(N) for c in range(2) if j != rank], key=order)
     slots = [(T.sb, T.sbp, 0), (T.own, T.ownp, 0), (T.own, T.ownp, 512)]
-    free = [0, 1, 1]
+    free = [0, 0, 0]
     full = [0, 0, 0]
     halves = [0] * N
-    count = [0]
+    blocks = []
 
     def products(j, c, s):
         codes, planes, col = slots[s]
@@ -183,55 +177,58 @@ def rank_program(g, core, T, topo):
                                      codes[:, b:b + 128], planes[:, b:b + 128],
                                      halves[j] == 1 and u == 0, halves[j] == 2 and u == 3)
         ins.then_inc(sem["f%d" % s], 1)
+        free[s] += 1
 
     def collect(j, s):
-        n = count[0]
-        count[0] = n + 1
-        h = n % 2
+        m = len(blocks)
+        h = m % 2
+        blocks.append(j)
         g.vector.wait_ge(sem["f%d" % s], free[s])
-        if n >= 2:
-            g.vector.wait_ge(sem["ys%d" % h], 16 * (n // 2))
+        if m >= 2:
+            g.vector.wait_ge(sem["ys%d" % h], 16 * (m // 2))
         g.vector.tensor_copy(T.yst[:, 128 * h:128 * h + 128], T.ps[:, 512 * j:512 * j + 128]).then_inc(sem["yc%d" % h], 1)
-        return n
+        return m
 
-    def store(j, n):
-        h = n % 2
-        g.scalar.wait_ge(sem["yc%d" % h], n // 2 + 1)
+    def store(j, m):
+        h = m % 2
+        g.scalar.wait_ge(sem["yc%d" % h], m // 2 + 1)
         g.scalar.dma_start(T.y[:, 128 * j:128 * j + 128], T.yst[:, 128 * h:128 * h + 128]).then_inc(sem["ys%d" % h], 16)
 
     g.tensor.wait_ge(sem.wl, 32)
-    quantised(g.tensor, 0)
-    products(rank, 0, 1)
-    quantised(g.tensor, 1)
-    products(rank, 1, 2)
-    store(rank, collect(rank, 2))
-    pend = []
+    for c in range(2):
+        quantised(g.tensor, c)
+        products(rank, c, 1 + c)
+    pend = [(rank, collect(rank, 2), -1)]
     for i, (j, c) in enumerate(items):
-        s = i % 3
+        p = (C0, C1)[c]
+        s = (0, 1, 0, 2)[i] if i < 4 else (1, 0, 2)[(i - 4) % 3]
         codes, planes, col = slots[s]
-        for q in (g.sync, g.scalar):
-            if free[s]:
-                q.wait_ge(sem["f%d" % s], free[s])
-            if s and i < 3:
-                q.wait_ge(sem["s%d" % (s - 1)], sent[s - 1])
-                q.wait_ge(sem["s%d" % PL], sent[PL])
-        arrived(g.sync, j, c)
-        g.sync.dma_start(codes[:, col:col + 512].bitcast(dt.uint8), land(j, c)).then_inc(sem["e%d" % s], 16)
+        if free[s]:
+            g.sync.wait_ge(sem["f%d" % s], free[s])
+            g.scalar.wait_ge(sem["f%d" % s], free[s])
+        if s and not full[s]:
+            g.sync.wait_ge(sem["s%d" % (C0, C1)[s - 1]], sent[(C0, C1)[s - 1]])
+            g.scalar.wait_ge(sem["s%d" % PL], sent[PL])
+        if i:
+            arrived(g.sync, j, p)
+            g.sync.dma_start(codes[:, col:col + 512].bitcast(dt.uint8), dram(j, p)).then_inc(sem["e%d" % s], 16)
+            full[s] += 16
+        else:
+            arrived(g.tensor, j, p)
         arrived(g.scalar, j, PL)
         g.scalar.dma_start(planes[:, col:col + 512], T["lp%d" % j][:, 512 * c:512 * c + 512]).then_inc(sem["e%d" % s], 16)
+        full[s] += 16
         while pend and pend[0][2] + 3 <= i:
             store(pend[0][0], pend[0][1])
             pend.pop(0)
-        full[s] += 32
         g.tensor.wait_ge(sem["e%d" % s], full[s])
         products(j, c, s)
-        free[s] += 1
         if halves[j] == 2:
             pend.append((j, collect(j, s), i))
-    for (j, n, i) in pend:
-        store(j, n)
+    for (j, m, i) in pend:
+        store(j, m)
     for q in (g.vector, g.scalar):
-        q.wait_ge(sem.ys0, 16 * ((N + 1) // 2))
+        q.wait_ge(sem.ys0, 16 * (N // 2))
         q.wait_ge(sem.ys1, 16 * (N // 2))
     for s in range(3):
         g.vector.wait_ge(sem["f%d" % s], free[s])

from concourse.bass import DstId, RemoteDMATransfer
from concourse.mybir import dt

CODES = "float8_e4m3fn_x4"
N = 8
SIM_CORES = 112
C0, PL, C1 = 0, 1, 2
PIECES = (C0, PL, C1)

SCRATCH = {
    "w": ("sbuf", [128, 1024], CODES), "wp": ("sbuf", [128, 1024], "uint8"),
    "own": ("sbuf", [128, 1024], CODES), "ownp": ("sbuf", [128, 1024], "uint8"),
    "sb": ("sbuf", [128, 512], CODES), "sbp": ("sbuf", [128, 512], "uint8"),
    "xin": ("sbuf", [128, 2048], "bfloat16"),
    "yst": ("sbuf", [128, 256], "float32"),
    "ps": ("psum", [128, 4096], "float32"),
}
for _j in range(N):
    SCRATCH["lc%d_%d" % (_j, C0)] = ("dram", [128, 512], CODES)
    SCRATCH["lc%d_%d" % (_j, C1)] = ("dram", [128, 512], CODES)
    SCRATCH["lp%d" % _j] = ("dram", [128, 1024], "uint8")

SEMAPHORES = (["a%d_%d" % (j, p) for j in range(N) for p in PIECES]
              + ["s%d" % p for p in PIECES] + ["sf", "wl"]
              + ["xl%d" % i for i in range(4)] + ["q%d" % i for i in range(4)]
              + ["f0", "f1", "f2", "e0", "e1", "e2", "yc0", "yc1", "ys0", "ys1"])


def ones(mask):
    return bin(mask).count("1")


def layout(T, topo):
    out = {}
    for ch in sorted(set(topo.chip(c) for c in T.cores)):
        far = [c for c in T.cores if topo.chip(c) != ch]

        def gate(c):
            return all(topo.may_write(c, d) for d in far)
        mine = [c for c in T.cores if topo.chip(c) == ch]
        rest = [c for c in range(SIM_CORES) if topo.chip(c) == ch and c not in mine]
        out[ch] = ([c for c in mine if not gate(c)], [c for c in mine if gate(c)],
                   [c for c in rest if not gate(c)], [c for c in rest if gate(c)])
    return out


def first_of(T, topo, core):
    ranks = [c for c in T.cores if topo.chip(c) == topo.chip(core)]
    return ranks[(ranks.index(core) + 1) % len(ranks)]


def build_plan(T, topo, lay):
    plan = {}
    way = {}

    def put(src, j, p, hop, trs):
        plan.setdefault(src, []).append((j, p, hop, trs))
        for dsts, mask in trs:
            for d in dsts:
                way[(d, j, p)] = mask
    for ch in lay:
        far = [c for c in lay if c != ch][0]
        inner, gates, _, ghelp = lay[ch]
        ranks, franks = inner + gates, lay[far][0] + lay[far][1]
        for src in ranks:
            j = T.rank_of(src)
            peers = [c for c in ranks if c != src]
            on = topo.mask(src, peers[0])
            k = (gates if src in gates else inner).index(src)
            for p in PIECES:
                if src in gates:
                    land = lay[far][0 if p == C1 else 2][k]
                    cross = topo.mask(src, land)
                    put(src, j, p, 0, [([land, peers[0]], cross), (peers[1:], on & ~cross)])
                    hop = 1.05
                else:
                    via, land = ghelp[k], lay[far][2][k]
                    put(src, j, p, 0, [([via] + peers, on)])
                    put(via, j, p, 1, [([land], topo.mask(via, land))])
                    hop = 2
                to = [c for c in franks if c != land]
                put(land, j, p, hop, [(to, topo.mask(land, to[0]))])
    return plan, way


def rank_program(g, core, T, topo):
    lay = layout(T, topo)
    plan, way = build_plan(T, topo, lay)
    if core not in plan:
        return
    rank = T.rank_of(core)
    sem = T.sem
    chip = topo.chip(core)

    def dram(j, p):
        return T["lp%d" % j][:, :] if p == PL else T["lc%d_%d" % (j, p)][:, :].bitcast(dt.uint8)

    def source(j, p):
        if j != rank:
            return dram(j, p)
        return T.ownp[:, :] if p == PL else T.own[:, 256 * p:256 * p + 512].bitcast(dt.uint8)

    def land(d, j, p):
        if p == C0 and T.rank_of(d) is not None and first_of(T, topo, d) == T.cores[j]:
            return T.sb[:, :].bitcast(dt.uint8)
        return dram(j, p)

    def dst_id(c):
        a = topo.addr(c)
        return DstId(rid=a[0], pnc=a[1])

    def arrived(q, j, p):
        q.wait_ge(sem["a%d_%d" % (j, p)], ones(way[(core, j, p)]))

    def quantised(q, half):
        q.wait_ge(sem["q%d" % (2 * half)], 2)
        q.wait_ge(sem["q%d" % (2 * half + 1)], 2)

    sent = {p: 0 for p in PIECES}
    passed = 0
    for j, p, hop, trs in sorted(plan[core], key=lambda w: (w[1] + 1.6 * w[2], w[0])):
        total = sum(ones(m) for (d, m) in trs)
        if j == rank:
            quantised(g, 0)
            if p != C0:
                quantised(g, 1)
            sent[p] += total
            ls = sem["s%d" % p]
        else:
            arrived(g, j, p)
            passed += total
            ls = sem.sf
        g.remote_dma_fused([RemoteDMATransfer(
            dst_ids=[dst_id(d) for d in dsts], dma_engine_mask=m, remote_sem=sem["a%d_%d" % (j, p)],
            srcs=[source(j, p)], dsts=[land(d, j, p) for d in dsts]) for (dsts, m) in trs], local_sem=ls)
    if passed:
        g.wait_ge(sem.sf, passed)
    if rank is None:
        return

    for i in range(4):
        q = g.sync if i % 2 == 0 else g.scalar
        h = 1024 * (i % 2)
        if i == 2:
            g.scalar.dma_start(T.wp[:, :], T.ws[:, :]).then_inc(sem.wl, 16)
            g.sync.dma_start(T.w[:, :].bitcast(dt.uint8), T.wc[:, :]).then_inc(sem.wl, 16)
        if i >= 2:
            q.wait_ge(sem["q%d" % (i - 2)], 2)
        q.dma_start(T.xin[:, h:h + 1024], T.x[:, 1024 * i:1024 * i + 1024]).then_inc(sem["xl%d" % i], 16)
    for i in range(4):
        g.vector.wait_ge(sem["xl%d" % i], 16)
        for t in (2 * i, 2 * i + 1):
            g.vector.quantize_mx(T.own[:, 128 * t:128 * t + 128], T.ownp[:, 128 * t:128 * t + 128],
                                 T.xin[:, 512 * (t % 4):512 * (t % 4) + 512]).then_inc(sem["q%d" % i], 1)

    first = T.rank_of(first_of(T, topo, core))

    def order(x):
        j, c = x
        inner = T.cores[j] in lay[topo.chip(T.cores[j])][0]
        if topo.chip(T.cores[j]) != chip:
            return (1, inner, j, c)
        return (0, j != first, c, inner, j)
    items = sorted([(j, c) for j in range(N) for c in range(2) if j != rank], key=order)
    slots = [(T.sb, T.sbp, 0), (T.own, T.ownp, 0), (T.own, T.ownp, 512)]
    free = [0, 0, 0]
    full = [0, 0, 0]
    halves = [0] * N
    blocks = []

    def products(j, c, s):
        codes, planes, col = slots[s]
        halves[j] += 1
        for u in range(4):
            a, b = 128 * (4 * c + u), col + 128 * u
            ins = g.tensor.matmul_mx(T.ps[:, 512 * j:512 * j + 128], T.w[:, a:a + 128], T.wp[:, a:a + 128],
                                     codes[:, b:b + 128], planes[:, b:b + 128],
                                     halves[j] == 1 and u == 0, halves[j] == 2 and u == 3)
        ins.then_inc(sem["f%d" % s], 1)
        free[s] += 1

    def collect(j, s):
        m = len(blocks)
        h = m % 2
        blocks.append(j)
        g.vector.wait_ge(sem["f%d" % s], free[s])
        if m >= 2:
            g.vector.wait_ge(sem["ys%d" % h], 16 * (m // 2))
        g.vector.tensor_copy(T.yst[:, 128 * h:128 * h + 128], T.ps[:, 512 * j:512 * j + 128]).then_inc(sem["yc%d" % h], 1)
        return m

    def store(j, m):
        h = m % 2
        g.scalar.wait_ge(sem["yc%d" % h], m // 2 + 1)
        g.scalar.dma_start(T.y[:, 128 * j:128 * j + 128], T.yst[:, 128 * h:128 * h + 128]).then_inc(sem["ys%d" % h], 16)

    g.tensor.wait_ge(sem.wl, 32)
    for c in range(2):
        quantised(g.tensor, c)
        products(rank, c, 1 + c)
    pend = [(rank, collect(rank, 2), -1)]
    for i, (j, c) in enumerate(items):
        p = (C0, C1)[c]
        s = (0, 1, 0, 2)[i] if i < 4 else (1, 0, 2)[(i - 4) % 3]
        codes, planes, col = slots[s]
        if free[s]:
            g.sync.wait_ge(sem["f%d" % s], free[s])
            g.scalar.wait_ge(sem["f%d" % s], free[s])
        if s and not full[s]:
            g.sync.wait_ge(sem["s%d" % (C0, C1)[s - 1]], sent[(C0, C1)[s - 1]])
            g.scalar.wait_ge(sem["s%d" % PL], sent[PL])
        if i:
            arrived(g.sync, j, p)
            g.sync.dma_start(codes[:, col:col + 512].bitcast(dt.uint8), dram(j, p)).then_inc(sem["e%d" % s], 16)
            full[s] += 16
        else:
            arrived(g.tensor, j, p)
        arrived(g.scalar, j, PL)
        g.scalar.dma_start(planes[:, col:col + 512], T["lp%d" % j][:, 512 * c:512 * c + 512]).then_inc(sem["e%d" % s], 16)
        full[s] += 16
        while pend and pend[0][2] + 3 <= i:
            store(pend[0][0], pend[0][1])
            pend.pop(0)
        g.tensor.wait_ge(sem["e%d" % s], full[s])
        products(j, c, s)
        if halves[j] == 2:
            pend.append((j, collect(j, s), i))
    for (j, m, i) in pend:
        store(j, m)
    for q in (g.vector, g.scalar):
        q.wait_ge(sem.ys0, 16 * (N // 2))
        q.wait_ge(sem.ys1, 16 * (N // 2))
    for s in range(3):
        g.vector.wait_ge(sem["f%d" % s], free[s])
